import numpy as np
import ml_dtypes


def mxq(x, axis, fmt="e4m3"):
    dtype, down = {"e4m3": (ml_dtypes.float8_e4m3fn, 7), "e5m2": (ml_dtypes.float8_e5m2, 14)}[fmt]
    v = np.moveaxis(np.asarray(x, np.float32).astype(ml_dtypes.bfloat16).astype(np.float64), axis, -1)
    blocks = v.reshape(v.shape[:-1] + (-1, 32))
    amax = np.abs(blocks).max(-1, keepdims=True)
    byte = np.maximum(np.where(amax > 0, np.frexp(amax)[1] - 1 + 127, 0) - down, 1)
    scale = np.exp2(byte - 127.0)
    codes = (blocks / scale).astype(np.float32).astype(dtype).astype(np.float64)
    return np.moveaxis((codes * scale).reshape(v.shape), -1, axis)


WIDE = False


def mx_kscale(k):
    if not WIDE:
        return np.ones(k)
    levels = np.array([10, -10, 5, -5, 0])
    if k % 512:
        return np.exp2(np.random.permutation(np.resize(levels, k // 32))).repeat(32)
    a = np.empty((k // 512, 16))
    for p in range(k // 512):
        a[p, :8] = np.random.permutation(np.resize(levels, 8))
        for g in range(8):
            far = levels[np.abs(levels - a[p, g]) >= 10]
            a[p, g + 8] = far[np.random.randint(len(far))]
    return np.exp2(a.ravel()).repeat(32)


def f64(x):
    return np.asarray(x).astype(np.float64)


def striped(idx):
    return np.tile(idx.reshape(-1, 16).T, (8, 1)).astype(np.uint16)


def unstriped(offs):
    return offs[:16].T.reshape(-1).astype(np.int64)


def pack_weight(w):
    k, n = w.shape
    w = f64(np.asarray(w, np.float32).astype(ml_dtypes.bfloat16)).reshape(k // 32, 32, n)
    amax = np.abs(w).max(1)
    byte = np.clip(np.where(amax > 0, np.frexp(amax)[1] - 1 + 127 - 7, 1), 1, 254)
    scaled = (w * np.exp2(127.0 - byte)[:, None, :]).reshape(k, n).astype(np.float32)
    words = np.ascontiguousarray(scaled.reshape(k // 512, 128, 4, n).transpose(0, 1, 3, 2)).astype(ml_dtypes.float8_e4m3fn).view(np.uint8)
    return words, np.ascontiguousarray(byte.astype(np.uint8).reshape(k // 512, 16, n))


def unpack_weight(words, scales):
    g, p, n, _ = words.shape
    vals = np.ascontiguousarray(words).view(ml_dtypes.float8_e4m3fn).astype(np.float64) * np.repeat(np.exp2(scales.astype(np.float64) - 127.0), 8, axis=1)[..., None]
    return vals.transpose(0, 1, 3, 2).reshape(g * 512, n)


E2M1 = np.array([0.0, 0.5, 1.0, 1.5, 2.0, 3.0, 4.0, 6.0, -0.0, -0.5, -1.0, -1.5, -2.0, -3.0, -4.0, -6.0])


def pack_fp4(w):
    k, n = w.shape
    w = f64(np.asarray(w, np.float32).astype(ml_dtypes.bfloat16)).reshape(k // 32, 32, n)
    amax = np.abs(w).max(1)
    mant, ex = np.frexp(amax / 6.0)
    byte = np.clip(np.where(amax > 0, np.where(mant > 0.5, ex, ex - 1) + 127, 1), 1, 254)
    scaled = (w * np.exp2(127.0 - byte)[:, None, :]).reshape(k, n).astype(np.float32)
    c = np.ascontiguousarray(scaled.reshape(k // 512, 128, 4, n).transpose(0, 1, 3, 2)).astype(ml_dtypes.float4_e2m1fn).view(np.uint8) & 0xF
    words = (c[..., 0::2] | (c[..., 1::2] << 4)).reshape(k // 512, 128, 2 * n)
    return np.ascontiguousarray(words), np.ascontiguousarray(byte.astype(np.uint8).reshape(k // 512, 16, n))


def unpack_fp4(words, scales):
    g, _, n = scales.shape
    words = np.ascontiguousarray(words).reshape(g, 128, n, 2)
    nib = np.empty((g, 128, n, 4), np.uint8)
    nib[..., 0::2] = words & 0xF
    nib[..., 1::2] = words >> 4
    vals = E2M1[nib] * np.repeat(np.exp2(scales.astype(np.float64) - 127.0), 8, axis=1)[..., None]
    return vals.transpose(0, 1, 3, 2).reshape(g * 512, n)


def planes(y):
    n, m = y.shape
    v = y.astype(np.float32).astype(ml_dtypes.bfloat16).astype(np.float64).reshape(n // 32, 32, m)
    top = np.abs(v).max(1)
    byte = np.clip(np.where(top > 0, np.frexp(top)[1] - 1 + 127 - 7, 1), 1, 254)
    codes = (v * np.exp2(127.0 - byte)[:, None, :]).reshape(n, m).astype(np.float32).astype(ml_dtypes.float8_e4m3fn).view(np.uint8)
    words = codes.reshape(n // 512, 128, 4, m).transpose(0, 1, 3, 2)
    return np.ascontiguousarray(words), np.ascontiguousarray(byte.astype(np.uint8).reshape(n // 512, 16, m))


K, T, S, N, H, V, U = 1024, 2048, 512, 512, 512, 256, 512


def setup_inputs():
    n = np.random.standard_normal
    s = mx_kscale(K)[:, None]
    u = mx_kscale(H)
    packed_xT = pack_weight(n((K, T)) * s)
    packed_w1 = pack_fp4(n((K, N)) / np.sqrt(K) / s)
    packed_w2 = pack_fp4(n((K, N)) / np.sqrt(K) / s)
    packed_w3 = pack_fp4(n((H, N)) / np.sqrt(H) / u[:, None])
    return {
        "x_words": packed_xT[0],
        "x_scales": packed_xT[1],
        "w1_words": packed_w1[0],
        "w1_scales": packed_w1[1],
        "w2_words": packed_w2[0],
        "w2_scales": packed_w2[1],
        "unit": (np.random.uniform(0.6, 1.4, (H, 1)) * u[:, None]).astype(np.float32),
        "w3_words": packed_w3[0],
        "w3_scales": packed_w3[1],
        "offs": striped(np.random.permutation(T)[:S]),
        "blk": striped(np.random.permutation(S)[:V]),
        "tok": striped(np.random.permutation(np.concatenate([np.arange(V), np.random.randint(0, V, U - V)]))),
        "req": striped(np.random.permutation(U)),
    }


def reference(x_words, x_scales, w1_words, w1_scales, w2_words, w2_scales, unit, w3_words, w3_scales, offs, blk, tok, req):
    xq = unpack_weight(x_words, x_scales)[:, unstriped(offs)]
    y = unpack_fp4(w1_words, w1_scales).T @ xq
    pk = y[:, unstriped(blk)]
    yv = unpack_fp4(w2_words, w2_scales).T @ xq
    pv = yv[:, unstriped(blk)]
    page = pk * np.tanh(pv)
    tk = page[:, unstriped(tok)]
    hid = f64(unit) * (np.maximum(tk, -0.8 * tk[:, unstriped(req)]))
    out_0 = unpack_fp4(w3_words, w3_scales).T @ mxq(hid, 0, "e4m3")
    return (out_0,) + planes(out_0)

@@ -1,0 +1,214 @@
+from contextlib import ExitStack
+
+import concourse.mybir as mybir
+
+K, T, S, H, V, U = 1024, 2048, 512, 512, 256, 512
+FLOPS = 2 * K * H * S * 2 + 2 * H * H * U
+
+F32 = mybir.dt.float32
+BF16 = mybir.dt.bfloat16
+I32 = mybir.dt.int32
+U32 = mybir.dt.uint32
+U16 = mybir.dt.uint16
+U8 = mybir.dt.uint8
+FP8X4 = mybir.dt.float8_e4m3fn_x4
+FP4X4 = mybir.dt.float4_e2m1fn_x4
+ALU = mybir.AluOpType
+ACT = mybir.ActivationFunctionType
+
+P = 128
+PACK = 4
+PASSES = K // (P * PACK)
+QUADS = 4
+WIDTHS = (256, 128, 128)
+BANK = 512
+
+
+def load_scale_rows(queue, plane, scales):
+    for q in range(QUADS):
+        queue.dma_start(
+            out=plane[32 * q : 32 * q + 4, :, :].bitcast(I32),
+            in_=scales[:, 4 * q : 4 * q + 4, :].rearrange("g r c -> r g c").bitcast(I32),
+        )
+
+
+def tile_picked_ypagetb_max_po_kernel(
+    tc, x_words, x_scales, w1_words, w1_scales, w2_words, w2_scales, unit, w3_words, w3_scales,
+    offs, blk, tok, req, out_0, out_1, out_2,
+):
+    nc = tc.nc
+    with ExitStack() as ctx:
+        keep = ctx.enter_context(tc.tile_pool(name="keep", bufs=1))
+        psum = ctx.enter_context(tc.psum_pool(name="psum", bufs=1))
+
+        def sb(name, shape, dtype):
+            return keep.tile(shape, dtype, name=name, align_bytes=64)
+
+        offs_sb = sb("offs_sb", [P, S // 16], U16)
+        blk_sb = sb("blk_sb", [P, V // 16], U16)
+        tok_sb = sb("tok_sb", [P, U // 16], U16)
+        req_sb = sb("req_sb", [P, U // 16], U16)
+        unit_sb = sb("unit_sb", [P, PACK], F32)
+        xw = [sb("xw%d" % g, [P, T], I32) for g in range(PASSES)]
+        xs = keep.tile([P, PASSES, T], U8, name="xs", tag="xs", align_bytes=64)
+        weights = [("w2", w2_words, w2_scales, PASSES), ("w1", w1_words, w1_scales, PASSES), ("w3", w3_words, w3_scales, 1)]
+        ww_raw = {n: sb(n + "w_raw", [P, g, 2 * H], U8) for n, w, s, g in weights}
+        ws_raw = {n: sb(n + "s_raw", [P, g, H], U8) for n, w, s, g in weights}
+        ww = {n: sb(n + "w", [P, g, PACK, 2 * P], U8) for n, w, s, g in weights}
+        ws = {n: sb(n + "s", [P, g, PACK, P], U8) for n, w, s, g in weights if n != "w1"}
+
+        nc.vector.memset(ws_raw["w2"][:].bitcast(I32), 0)
+        nc.vector.memset(xs[:].bitcast(I32), 0)
+        nc.vector.memset(ws_raw["w1"][:].bitcast(I32), 0)
+        nc.vector.memset(ws_raw["w3"][:].bitcast(I32), 0)
+
+        def load_words(n, w):
+            nc.sync.dma_start(out=ww_raw[n][:].bitcast(I32), in_=w.rearrange("g p c -> p g c").bitcast(I32))
+
+        def load_x(g):
+            nc.sync.dma_start(out=xw[g][:], in_=x_words[g].rearrange("p c r -> p (c r)").bitcast(I32))
+
+        nc.sync.dma_start(offs_sb[:], offs)
+        load_x(0)
+        nc.gpsimd.dma_start(out=unit_sb[:], in_=unit.rearrange("(p t) o -> p (t o)", t=PACK))
+        load_scale_rows(nc.gpsimd, xs, x_scales)
+        load_scale_rows(nc.scalar, ws_raw["w2"], w2_scales)
+        sign = sb("sign", [P, 2, 2], BF16)
+        size = sb("size", [P, PACK], F32)
+        nc.scalar.activation(size[:], unit_sb[:], ACT.Abs)
+        nc.scalar.activation(sign[:].rearrange("p u e -> p (u e)"), unit_sb[:], ACT.Sign)
+        load_words("w2", w2_words)
+        load_words("w1", w1_words)
+        load_x(1)
+        load_scale_rows(nc.scalar, ws_raw["w1"], w1_scales)
+        load_words("w3", w3_words)
+        nc.sync.dma_start(blk_sb[:], blk)
+        nc.sync.dma_start(tok_sb[:], tok)
+        nc.sync.dma_start(req_sb[:], req)
+        load_scale_rows(nc.gpsimd, ws_raw["w3"], w3_scales)
+
+        def deal_words(n, ts):
+            nc.scalar.copy(
+                out=ww[n][:, :, ts, :].bitcast(U16),
+                in_=ww_raw[n][:].bitcast(U16).rearrange("p g (m t) -> p g t m", t=PACK)[:, :, ts, :],
+            )
+
+        def deal_scales(n, ts):
+            nc.vector.tensor_copy(out=ws[n][:, :, ts, :], in_=ws_raw[n][:].rearrange("p g (m t) -> p g t m", t=PACK)[:, :, ts, :])
+
+        gw = [sb("gw%d" % g, [P, S], U32) for g in range(PASSES)]
+        gs = [sb("gs%d" % g, [P, S], U8) for g in range(PASSES)]
+
+        def gather_words(g):
+            nc.vector.tensor_copy(gw[g][:], xw[g][:].bitcast(U32).indirect(offs_sb[:]))
+
+        def gather_scales(g):
+            nc.vector.tensor_copy(gs[g][:], xs[:, g, :].indirect(offs_sb[:]))
+
+        deal_scales("w2", slice(0, PACK))
+        gather_words(0)
+        gather_scales(0)
+        gather_scales(1)
+        ws["w1"] = keep.tile([P, PASSES, PACK, P], U8, name="w1s", tag="xs", align_bytes=64)
+        deal_scales("w1", slice(0, 1))
+        gather_words(1)
+        deal_scales("w1", slice(1, PACK))
+        for ts in (slice(0, 2), slice(2, PACK)):
+            deal_words("w2", ts)
+            deal_words("w1", ts)
+        deal_words("w3", slice(0, PACK))
+
+        acc = {}
+        for t in range(PACK):
+            for n in ("w2", "w1"):
+                acc[n, t] = psum.tile([P, S], F32, name="acc_%s_%d" % (n, t), tag="bank_%s_%d" % (n, t))
+        for t in range(PACK):
+            for g in range(PASSES):
+                for n in ("w2", "w1"):
+                    nc.tensor.matmul_mx(
+                        out=acc[n, t][:],
+                        lhsT=ww[n][:, g, t, :].bitcast(FP4X4),
+                        lhsT_scale=ws[n][:, g, t, :],
+                        rhs=gw[g][:].bitcast(FP8X4),
+                        rhs_scale=gs[g][:],
+                        start=(g == 0),
+                        stop=(g == PASSES - 1),
+                    )
+
+        bounded = [sb("bounded%d" % t, [P, S], F32) for t in range(PACK)]
+        pages = [sb("pages%d" % t, [P, V + S], F32) for t in range(PACK)]
+        tk = [sb("tk%d" % u, [P, 2, U], F32) for u in range(2)]
+        copy_on = {"V": nc.vector.tensor_copy, "S": lambda o, i: nc.scalar.activation(o, i, ACT.Copy)}
+
+        for t in range(PACK):
+            nc.scalar.activation(bounded[t][:], acc["w2", t][:], ACT.Tanh)
+        for t in range(PACK):
+            nc.vector.scalar_tensor_tensor(
+                pages[t][:, V:], acc["w1", t][:], size[:, t : t + 1], bounded[t][:], ALU.mult, ALU.mult
+            )
+            nc.vector.tensor_copy(pages[t][:, :V], pages[t][:, V:].indirect(blk_sb[:]))
+            copy_on["V" if t == PACK - 1 else "S"](tk[t // 2][:, t % 2, :], pages[t][:].indirect(tok_sb[:]))
+
+        deal_scales("w3", slice(0, PACK))
+
+        out_words = sb("out_words", [P, U], U32)
+        out_scales = sb("out_scales", [P, U], U8)
+        out_rows = out_0.rearrange("(p t) j -> p t j", t=PACK)
+        words_dram = out_1[0].rearrange("p c r -> p (c r)").bitcast(I32)
+        free_banks = ["bank_%s_%d" % (n, t) for t in range(PACK) for n in ("w2", "w1")]
+        first = 0
+        for q, width in enumerate(WIDTHS):
+            cols = slice(first, first + width)
+            picks = req_sb[:, first // 16 : (first + width) // 16]
+            first = first + width
+            other = sb("other%d" % q, [P, PACK, width], F32)
+            for t in range(PACK):
+                copy_on["V" if t == 0 else "S"](other[:, t, :], tk[t // 2][:, t % 2, :].indirect(picks))
+            pairs = sb("pairs%d" % q, [P, 2, width, 2], BF16)
+            for u in range(2):
+                nc.vector.scalar_tensor_tensor(
+                    pairs[:, u, :, :],
+                    other[:, 2 * u : 2 * u + 2, :].rearrange("p e c -> p c e"),
+                    -0.8,
+                    tk[u][:, :, cols].rearrange("p e c -> p c e"),
+                    ALU.mult,
+                    ALU.max,
+                )
+            hid = sb("hid%d" % q, [P, width, 2, 2], BF16)
+            nc.vector.tensor_tensor(
+                hid[:],
+                pairs[:].rearrange("p u c e -> p c u e"),
+                sign[:].unsqueeze(1).to_broadcast([P, width, 2, 2]),
+                ALU.mult,
+            )
+            hid_words = sb("hid_words%d" % q, [P, width], U32)
+            hid_scales = sb("hid_scales%d" % q, [P, width], U8)
+            nc.vector.quantize_mx(
+                out=hid_words[:].bitcast(FP8X4), scales=hid_scales[:], in_=hid[:].rearrange("p c u e -> p (c u e)")
+            )
+            res32 = sb("res32_%d" % q, [P, PACK, width], F32)
+            per_bank = BANK // width
+            for t0 in range(0, PACK, per_bank):
+                res = psum.tile([P, per_bank, width], F32, name="res%d_%d" % (q, t0), tag=free_banks.pop(0))
+                for t in range(t0, t0 + per_bank):
+                    nc.tensor.matmul_mx(
+                        out=res[:, t - t0, :],
+                        lhsT=ww["w3"][:, 0, t, :].bitcast(FP4X4),
+                        lhsT_scale=ws["w3"][:, 0, t, :],
+                        rhs=hid_words[:].bitcast(FP8X4),
+                        rhs_scale=hid_scales[:],
+                        start=True,
+                        stop=True,
+                    )
+                nc.scalar.copy(res32[:, t0 : t0 + per_bank, :], res[:])
+            nc.sync.dma_start(out=out_rows[:, :, cols], in_=res32[:])
+            res16 = sb("res16_%d" % q, [P, width, PACK], BF16)
+            nc.vector.tensor_copy(res16[:], res32[:].rearrange("p t c -> p c t"))
+            nc.vector.quantize_mx(
+                out=out_words[:, cols].bitcast(FP8X4), scales=out_scales[:, cols], in_=res16[:].rearrange("p c t -> p (c t)")
+            )
+            nc.sync.dma_start(out=words_dram[:, cols], in_=out_words[:, cols].bitcast(I32))
+        for q in range(QUADS):
+            (nc.sync if q % 2 else nc.scalar).dma_start(
+                out=out_2[0, 4 * q : 4 * q + 4, :].bitcast(I32), in_=out_scales[32 * q : 32 * q + 4, :].bitcast(I32)
+            )

@@ -20,14 +20,18 @@ P = 128
 PACK = 4
 PASSES = K // (P * PACK)
 QUADS = 4
-WIDTHS = (256, 128, 128)
+WIDTHS = (128, 128, 128, 128)
+BLK_ON = "SVVV"
+TOK_ON = "SSSV"
+REQ_ON = ("VSSS", "VSSS", "VSSS", "VSSS")
+ROUND_ON = "VVVV"
 BANK = 512
 
 
-def load_scale_rows(queue, plane, scales):
+def load_scale_rows(nc, planes, scales):
     for q in range(QUADS):
-        queue.dma_start(
-            out=plane[32 * q : 32 * q + 4, :, :].bitcast(I32),
+        nc.sync.dma_start(
+            out=planes[32 * q : 32 * q + 4, :, :].bitcast(I32),
             in_=scales[:, 4 * q : 4 * q + 4, :].rearrange("g r c -> r g c").bitcast(I32),
         )
 
@@ -50,17 +54,20 @@ def tile_picked_ypagetb_max_po_kernel(
         req_sb = sb("req_sb", [P, U // 16], U16)
         unit_sb = sb("unit_sb", [P, PACK], F32)
         xw = [sb("xw%d" % g, [P, T], I32) for g in range(PASSES)]
-        xs = keep.tile([P, PASSES, T], U8, name="xs", tag="xs", align_bytes=64)
-        weights = [("w2", w2_words, w2_scales, PASSES), ("w1", w1_words, w1_scales, PASSES), ("w3", w3_words, w3_scales, 1)]
-        ww_raw = {n: sb(n + "w_raw", [P, g, 2 * H], U8) for n, w, s, g in weights}
-        ws_raw = {n: sb(n + "s_raw", [P, g, H], U8) for n, w, s, g in weights}
-        ww = {n: sb(n + "w", [P, g, PACK, 2 * P], U8) for n, w, s, g in weights}
-        ws = {n: sb(n + "s", [P, g, PACK, P], U8) for n, w, s, g in weights if n != "w1"}
+        xs = sb("xs", [P, PASSES, T], U8)
+        passes_of = {"w1": PASSES, "w2": PASSES, "w3": 1}
+        ww_raw = {n: sb(n + "w_raw", [P, g, 2 * H], U8) for n, g in passes_of.items()}
+        ww = {n: sb(n + "w", [P, PACK, g, 2 * P], U8) for n, g in passes_of.items()}
+        s21_raw = sb("s21_raw", [P, 2 * PASSES, H], U8)
+        s3_raw = sb("s3_raw", [P, 1, H], U8)
+        s_first = sb("s_first", [P, PACK, P], U8)
+        s_rest = sb("s_rest", [P, PACK, 2 * PASSES - 1, P], U8)
+        s3 = sb("s3", [P, PACK, P], U8)
 
-        nc.vector.memset(ws_raw["w2"][:].bitcast(I32), 0)
+        nc.gpsimd.memset(s21_raw[:, :PASSES, :].bitcast(I32), 0)
         nc.vector.memset(xs[:].bitcast(I32), 0)
-        nc.vector.memset(ws_raw["w1"][:].bitcast(I32), 0)
-        nc.vector.memset(ws_raw["w3"][:].bitcast(I32), 0)
+        nc.vector.memset(s21_raw[:, PASSES:, :].bitcast(I32), 0)
+        nc.vector.memset(s3_raw[:].bitcast(I32), 0)
 
         def load_words(n, w):
             nc.sync.dma_start(out=ww_raw[n][:].bitcast(I32), in_=w.rearrange("g p c -> p g c").bitcast(I32))
@@ -69,32 +76,37 @@ def tile_picked_ypagetb_max_po_kernel(
             nc.sync.dma_start(out=xw[g][:], in_=x_words[g].rearrange("p c r -> p (c r)").bitcast(I32))
 
         nc.sync.dma_start(offs_sb[:], offs)
+        nc.scalar.dma_start(out=unit_sb[:], in_=unit.rearrange("(p t) o -> p (t o)", t=PACK))
+        load_scale_rows(nc, s21_raw[:, :PASSES, :], w2_scales)
         load_x(0)
-        nc.gpsimd.dma_start(out=unit_sb[:], in_=unit.rearrange("(p t) o -> p (t o)", t=PACK))
-        load_scale_rows(nc.gpsimd, xs, x_scales)
-        load_scale_rows(nc.scalar, ws_raw["w2"], w2_scales)
+        load_scale_rows(nc, xs, x_scales)
+        load_words("w2", w2_words)
+        load_x(1)
+        load_words("w1", w1_words)
+        load_scale_rows(nc, s21_raw[:, PASSES:, :], w1_scales)
+        nc.sync.dma_start(blk_sb[:], blk)
+        nc.sync.dma_start(tok_sb[:], tok)
+        load_words("w3", w3_words)
+        nc.sync.dma_start(req_sb[:], req)
+        load_scale_rows(nc, s3_raw, w3_scales)
+
         sign = sb("sign", [P, 2, 2], BF16)
         size = sb("size", [P, PACK], F32)
         nc.scalar.activation(size[:], unit_sb[:], ACT.Abs)
         nc.scalar.activation(sign[:].rearrange("p u e -> p (u e)"), unit_sb[:], ACT.Sign)
-        load_words("w2", w2_words)
-        load_words("w1", w1_words)
-        load_x(1)
-        load_scale_rows(nc.scalar, ws_raw["w1"], w1_scales)
-        load_words("w3", w3_words)
-        nc.sync.dma_start(blk_sb[:], blk)
-        nc.sync.dma_start(tok_sb[:], tok)
-        nc.sync.dma_start(req_sb[:], req)
-        load_scale_rows(nc.gpsimd, ws_raw["w3"], w3_scales)
 
         def deal_words(n, ts):
             nc.scalar.copy(
-                out=ww[n][:, :, ts, :].bitcast(U16),
-                in_=ww_raw[n][:].bitcast(U16).rearrange("p g (m t) -> p g t m", t=PACK)[:, :, ts, :],
+                out=ww[n][:, ts, :, :].bitcast(U16),
+                in_=ww_raw[n][:].bitcast(U16).rearrange("p g (m t) -> p t g m", t=PACK)[:, ts, :, :],
             )
 
-        def deal_scales(n, ts):
-            nc.vector.tensor_copy(out=ws[n][:, :, ts, :], in_=ws_raw[n][:].rearrange("p g (m t) -> p g t m", t=PACK)[:, :, ts, :])
+        s21_dealt = s21_raw[:].rearrange("p g (m t) -> p t g m", t=PACK)
+
+        def deal_rest(ts, first_plane, last_plane):
+            nc.vector.tensor_copy(
+                out=s_rest[:, ts, first_plane - 1 : last_plane, :], in_=s21_dealt[:, ts, first_plane : last_plane + 1, :]
+            )
 
         gw = [sb("gw%d" % g, [P, S], U32) for g in range(PASSES)]
         gs = [sb("gs%d" % g, [P, S], U8) for g in range(PASSES)]
@@ -105,35 +117,42 @@ def tile_picked_ypagetb_max_po_kernel(
         def gather_scales(g):
             nc.vector.tensor_copy(gs[g][:], xs[:, g, :].indirect(offs_sb[:]))
 
-        deal_scales("w2", slice(0, PACK))
+        nc.vector.tensor_copy(out=s_first[:], in_=s21_dealt[:, :, 0, :])
+        deal_rest(slice(0, 1), 1, 1)
+        deal_words("w2", slice(0, PACK))
         gather_words(0)
         gather_scales(0)
         gather_scales(1)
-        ws["w1"] = keep.tile([P, PASSES, PACK, P], U8, name="w1s", tag="xs", align_bytes=64)
-        deal_scales("w1", slice(0, 1))
         gather_words(1)
-        deal_scales("w1", slice(1, PACK))
-        for ts in (slice(0, 2), slice(2, PACK)):
-            deal_words("w2", ts)
+        deal_rest(slice(0, 1), 2, 3)
+        deal_words("w1", slice(0, 1))
+        for ts in (slice(1, 2), slice(2, PACK)):
+            deal_rest(ts, 1, 3)
             deal_words("w1", ts)
-        deal_words("w3", slice(0, PACK))
 
         acc = {}
         for t in range(PACK):
             for n in ("w2", "w1"):
                 acc[n, t] = psum.tile([P, S], F32, name="acc_%s_%d" % (n, t), tag="bank_%s_%d" % (n, t))
+
+        def product_pass(n, t, g):
+            plane = g if n == "w2" else PASSES + g
+            nc.tensor.matmul_mx(
+                out=acc[n, t][:],
+                lhsT=ww[n][:, t, g, :].bitcast(FP4X4),
+                lhsT_scale=s_first[:, t, :] if plane == 0 else s_rest[:, t, plane - 1, :],
+                rhs=gw[g][:].bitcast(FP8X4),
+                rhs_scale=gs[g][:],
+                start=(g == 0),
+                stop=(g == PASSES - 1),
+            )
+
         for t in range(PACK):
-            for g in range(PASSES):
-                for n in ("w2", "w1"):
-                    nc.tensor.matmul_mx(
-                        out=acc[n, t][:],
-                        lhsT=ww[n][:, g, t, :].bitcast(FP4X4),
-                        lhsT_scale=ws[n][:, g, t, :],
-                        rhs=gw[g][:].bitcast(FP8X4),
-                        rhs_scale=gs[g][:],
-                        start=(g == 0),
-                        stop=(g == PASSES - 1),
-                    )
+            product_pass("w2", t, 0)
+        for t in range(PACK):
+            product_pass("w2", t, 1)
+            product_pass("w1", t, 0)
+            product_pass("w1", t, 1)
 
         bounded = [sb("bounded%d" % t, [P, S], F32) for t in range(PACK)]
         pages = [sb("pages%d" % t, [P, V + S], F32) for t in range(PACK)]
@@ -146,24 +165,28 @@ def tile_picked_ypagetb_max_po_kernel(
             nc.vector.scalar_tensor_tensor(
                 pages[t][:, V:], acc["w1", t][:], size[:, t : t + 1], bounded[t][:], ALU.mult, ALU.mult
             )
-            nc.vector.tensor_copy(pages[t][:, :V], pages[t][:, V:].indirect(blk_sb[:]))
-            copy_on["V" if t == PACK - 1 else "S"](tk[t // 2][:, t % 2, :], pages[t][:].indirect(tok_sb[:]))
+            copy_on[BLK_ON[t]](pages[t][:, :V], pages[t][:, V:].indirect(blk_sb[:]))
+        for t in range(PACK):
+            copy_on[TOK_ON[t]](tk[t // 2][:, t % 2, :], pages[t][:].indirect(tok_sb[:]))
 
-        deal_scales("w3", slice(0, PACK))
+        deal_words("w3", slice(0, PACK))
+        nc.vector.tensor_copy(out=s3[:], in_=s3_raw[:, 0, :].rearrange("p (m t) -> p t m", t=PACK))
 
         out_words = sb("out_words", [P, U], U32)
         out_scales = sb("out_scales", [P, U], U8)
         out_rows = out_0.rearrange("(p t) j -> p t j", t=PACK)
         words_dram = out_1[0].rearrange("p c r -> p (c r)").bitcast(I32)
         free_banks = ["bank_%s_%d" % (n, t) for t in range(PACK) for n in ("w2", "w1")]
-        first = 0
-        for q, width in enumerate(WIDTHS):
-            cols = slice(first, first + width)
-            picks = req_sb[:, first // 16 : (first + width) // 16]
-            first = first + width
+        starts = [sum(WIDTHS[:q]) for q in range(len(WIDTHS))]
+        results = {}
+
+        def front(q):
+            width = WIDTHS[q]
+            cols = slice(starts[q], starts[q] + width)
+            picks = req_sb[:, cols.start // 16 : cols.stop // 16]
             other = sb("other%d" % q, [P, PACK, width], F32)
             for t in range(PACK):
-                copy_on["V" if t == 0 else "S"](other[:, t, :], tk[t // 2][:, t % 2, :].indirect(picks))
+                copy_on[REQ_ON[q][t]](other[:, t, :], tk[t // 2][:, t % 2, :].indirect(picks))
             pairs = sb("pairs%d" % q, [P, 2, width, 2], BF16)
             for u in range(2):
                 nc.vector.scalar_tensor_tensor(
@@ -186,28 +209,44 @@ def tile_picked_ypagetb_max_po_kernel(
             nc.vector.quantize_mx(
                 out=hid_words[:].bitcast(FP8X4), scales=hid_scales[:], in_=hid[:].rearrange("p c u e -> p (c u e)")
             )
-            res32 = sb("res32_%d" % q, [P, PACK, width], F32)
             per_bank = BANK // width
+            results[q] = []
             for t0 in range(0, PACK, per_bank):
                 res = psum.tile([P, per_bank, width], F32, name="res%d_%d" % (q, t0), tag=free_banks.pop(0))
+                results[q].append(res)
                 for t in range(t0, t0 + per_bank):
                     nc.tensor.matmul_mx(
                         out=res[:, t - t0, :],
-                        lhsT=ww["w3"][:, 0, t, :].bitcast(FP4X4),
-                        lhsT_scale=ws["w3"][:, 0, t, :],
+                        lhsT=ww["w3"][:, t, 0, :].bitcast(FP4X4),
+                        lhsT_scale=s3[:, t, :],
                         rhs=hid_words[:].bitcast(FP8X4),
                         rhs_scale=hid_scales[:],
                         start=True,
                         stop=True,
                     )
-                nc.scalar.copy(res32[:, t0 : t0 + per_bank, :], res[:])
-            nc.sync.dma_start(out=out_rows[:, :, cols], in_=res32[:])
+
+        def back(q):
+            width = WIDTHS[q]
+            cols = slice(starts[q], starts[q] + width)
+            per_bank = BANK // width
+            res32 = sb("res32_%d" % q, [P, PACK, width], F32)
             res16 = sb("res16_%d" % q, [P, width, PACK], BF16)
-            nc.vector.tensor_copy(res16[:], res32[:].rearrange("p t c -> p c t"))
+            for i, res in enumerate(results[q]):
+                if ROUND_ON[q] == "S":
+                    nc.scalar.copy(res16[:], res[:].rearrange("p t c -> p c t"))
+                nc.scalar.copy(res32[:, i * per_bank : (i + 1) * per_bank, :], res[:])
+            nc.sync.dma_start(out=out_rows[:, :, cols], in_=res32[:])
+            if ROUND_ON[q] == "V":
+                nc.vector.tensor_copy(res16[:], res32[:].rearrange("p t c -> p c t"))
             nc.vector.quantize_mx(
                 out=out_words[:, cols].bitcast(FP8X4), scales=out_scales[:, cols], in_=res16[:].rearrange("p c t -> p (c t)")
             )
             nc.sync.dma_start(out=words_dram[:, cols], in_=out_words[:, cols].bitcast(I32))
+
+        for q in range(len(WIDTHS)):
+            front(q)
+        for q in range(len(WIDTHS)):
+            back(q)
         for q in range(QUADS):
             (nc.sync if q % 2 else nc.scalar).dma_start(
                 out=out_2[0, 4 * q : 4 * q + 4, :].bitcast(I32), in_=out_scales[32 * q : 32 * q + 4, :].bitcast(I32)

@@ -21,10 +21,9 @@ PACK = 4
 PASSES = K // (P * PACK)
 QUADS = 4
 WIDTHS = (128, 128, 128, 128)
-BLK_ON = "SVVV"
-TOK_ON = "SSSV"
-REQ_ON = ("VSSS", "VSSS", "VSSS", "VSSS")
-ROUND_ON = "VVVV"
+BLK_ON = "SSVV"
+TOK_ON = "VSVV"
+ROUND_ON = "SVVV"
 BANK = 512
 
 
@@ -179,22 +178,25 @@ def tile_picked_ypagetb_max_po_kernel(
         free_banks = ["bank_%s_%d" % (n, t) for t in range(PACK) for n in ("w2", "w1")]
         starts = [sum(WIDTHS[:q]) for q in range(len(WIDTHS))]
         results = {}
+        others = {}
 
         def front(q):
             width = WIDTHS[q]
             cols = slice(starts[q], starts[q] + width)
-            picks = req_sb[:, cols.start // 16 : cols.stop // 16]
-            other = sb("other%d" % q, [P, PACK, width], F32)
-            for t in range(PACK):
-                copy_on[REQ_ON[q][t]](other[:, t, :], tk[t // 2][:, t % 2, :].indirect(picks))
+            if q % 2 == 0:
+                picks = req_sb[:, cols.start // 16 : (cols.start + 2 * width) // 16]
+                others[q // 2] = sb("other%d" % q, [P, PACK, 2 * width], F32)
+                for t in range(PACK):
+                    nc.scalar.activation(
+                        others[q // 2][:, t, :], tk[t // 2][:, t % 2, :].indirect(picks), ACT.Copy, scale=-0.8
+                    )
+            other = others[q // 2][:, :, q % 2 * width : (q % 2 + 1) * width]
             pairs = sb("pairs%d" % q, [P, 2, width, 2], BF16)
             for u in range(2):
-                nc.vector.scalar_tensor_tensor(
-                    pairs[:, u, :, :],
-                    other[:, 2 * u : 2 * u + 2, :].rearrange("p e c -> p c e"),
-                    -0.8,
-                    tk[u][:, :, cols].rearrange("p e c -> p c e"),
-                    ALU.mult,
+                nc.vector.tensor_tensor(
+                    pairs[:, u, :, :].rearrange("p (c i) e -> p c e i", i=4),
+                    other[:, 2 * u : 2 * u + 2, :].rearrange("p e (c i) -> p c e i", i=4),
+                    tk[u][:, :, cols].rearrange("p e (c i) -> p c e i", i=4),
                     ALU.max,
                 )
             hid = sb("hid%d" % q, [P, width, 2, 2], BF16)
@@ -237,7 +239,9 @@ def tile_picked_ypagetb_max_po_kernel(
                 nc.scalar.copy(res32[:, i * per_bank : (i + 1) * per_bank, :], res[:])
             nc.sync.dma_start(out=out_rows[:, :, cols], in_=res32[:])
             if ROUND_ON[q] == "V":
-                nc.vector.tensor_copy(res16[:], res32[:].rearrange("p t c -> p c t"))
+                nc.vector.tensor_copy(
+                    res16[:].rearrange("p (c i) t -> p c t i", i=4), res32[:].rearrange("p t (c i) -> p c t i", i=4)
+                )
             nc.vector.quantize_mx(
                 out=out_words[:, cols].bitcast(FP8X4), scales=out_scales[:, cols], in_=res16[:].rearrange("p c t -> p (c t)")
             )

@@ -28,11 +28,9 @@ BANK = 512
 
 
 def load_scale_rows(nc, planes, scales):
-    for q in range(QUADS):
-        nc.sync.dma_start(
-            out=planes[32 * q : 32 * q + 4, :, :].bitcast(I32),
-            in_=scales[:, 4 * q : 4 * q + 4, :].rearrange("g r c -> r g c").bitcast(I32),
-        )
+    rows = scales.rearrange("g (q r) c -> r q g c", r=4)
+    for r in range(4):
+        nc.sync.dma_start(out=planes[r:P:32, :, :].bitcast(I32), in_=rows[r].bitcast(I32))
 
 
 def tile_picked_ypagetb_max_po_kernel(
@@ -56,7 +54,11 @@ def tile_picked_ypagetb_max_po_kernel(
         xs = sb("xs", [P, PASSES, T], U8)
         passes_of = {"w1": PASSES, "w2": PASSES, "w3": 1}
         ww_raw = {n: sb(n + "w_raw", [P, g, 2 * H], U8) for n, g in passes_of.items()}
-        ww = {n: sb(n + "w", [P, PACK, g, 2 * P], U8) for n, g in passes_of.items()}
+        ww = {
+            "w1": sb("w1w", [P, PACK, PASSES, 2 * P], U8)[:],
+            "w2": sb("w2w", [P, PASSES, PACK, 2 * P], U8)[:].rearrange("p g t m -> p t g m"),
+            "w3": sb("w3w", [P, PACK, 1, 2 * P], U8)[:],
+        }
         s21_raw = sb("s21_raw", [P, 2 * PASSES, H], U8)
         s3_raw = sb("s3_raw", [P, 1, H], U8)
         s_first = sb("s_first", [P, PACK, P], U8)
@@ -78,8 +80,8 @@ def tile_picked_ypagetb_max_po_kernel(
         nc.scalar.dma_start(out=unit_sb[:], in_=unit.rearrange("(p t) o -> p (t o)", t=PACK))
         load_scale_rows(nc, s21_raw[:, :PASSES, :], w2_scales)
         load_x(0)
-        load_scale_rows(nc, xs, x_scales)
         load_words("w2", w2_words)
+        load_scale_rows(nc, xs, x_scales)
         load_x(1)
         load_words("w1", w1_words)
         load_scale_rows(nc, s21_raw[:, PASSES:, :], w1_scales)
@@ -94,10 +96,10 @@ def tile_picked_ypagetb_max_po_kernel(
         nc.scalar.activation(size[:], unit_sb[:], ACT.Abs)
         nc.scalar.activation(sign[:].rearrange("p u e -> p (u e)"), unit_sb[:], ACT.Sign)
 
-        def deal_words(n, ts):
+        def deal_words(n, ts, passes=slice(0, PASSES)):
             nc.scalar.copy(
-                out=ww[n][:, ts, :, :].bitcast(U16),
-                in_=ww_raw[n][:].bitcast(U16).rearrange("p g (m t) -> p t g m", t=PACK)[:, ts, :, :],
+                out=ww[n][:, ts, passes, :].bitcast(U16),
+                in_=ww_raw[n][:].bitcast(U16).rearrange("p g (m t) -> p t g m", t=PACK)[:, ts, passes, :],
             )
 
         s21_dealt = s21_raw[:].rearrange("p g (m t) -> p t g m", t=PACK)
@@ -118,7 +120,8 @@ def tile_picked_ypagetb_max_po_kernel(
 
         nc.vector.tensor_copy(out=s_first[:], in_=s21_dealt[:, :, 0, :])
         deal_rest(slice(0, 1), 1, 1)
-        deal_words("w2", slice(0, PACK))
+        deal_words("w2", slice(0, PACK), slice(0, 1))
+        deal_words("w2", slice(0, PACK), slice(1, 2))
         gather_words(0)
         gather_scales(0)
         gather_scales(1)
@@ -168,7 +171,7 @@ def tile_picked_ypagetb_max_po_kernel(
         for t in range(PACK):
             copy_on[TOK_ON[t]](tk[t // 2][:, t % 2, :], pages[t][:].indirect(tok_sb[:]))
 
-        deal_words("w3", slice(0, PACK))
+        deal_words("w3", slice(0, PACK), slice(0, 1))
         nc.vector.tensor_copy(out=s3[:], in_=s3_raw[:, 0, :].rearrange("p (m t) -> p t m", t=PACK))
 
         out_words = sb("out_words", [P, U], U32)
@@ -251,7 +254,8 @@ def tile_picked_ypagetb_max_po_kernel(
             front(q)
         for q in range(len(WIDTHS)):
             back(q)
-        for q in range(QUADS):
-            (nc.sync if q % 2 else nc.scalar).dma_start(
-                out=out_2[0, 4 * q : 4 * q + 4, :].bitcast(I32), in_=out_scales[32 * q : 32 * q + 4, :].bitcast(I32)
+        scale_rows = out_2[0].rearrange("(q r) c -> r q c", r=4)
+        for r in range(4):
+            (nc.sync if r % 2 else nc.scalar).dma_start(
+                out=scale_rows[r].bitcast(I32), in_=out_scales[r:P:32, :].bitcast(I32)
             )

from contextlib import ExitStack

import concourse.mybir as mybir

K, T, S, H, V, U = 1024, 2048, 512, 512, 256, 512
FLOPS = 2 * K * H * S * 2 + 2 * H * H * U

F32 = mybir.dt.float32
BF16 = mybir.dt.bfloat16
I32 = mybir.dt.int32
U32 = mybir.dt.uint32
U16 = mybir.dt.uint16
U8 = mybir.dt.uint8
FP8X4 = mybir.dt.float8_e4m3fn_x4
FP4X4 = mybir.dt.float4_e2m1fn_x4
ALU = mybir.AluOpType
ACT = mybir.ActivationFunctionType

P = 128
PACK = 4
PASSES = K // (P * PACK)
QUADS = 4
WIDTHS = (128, 128, 128, 128)
BLK_ON = "SSVV"
TOK_ON = "VSVV"
ROUND_ON = "SVVV"
BANK = 512


def load_scale_rows(nc, planes, scales):
    rows = scales.rearrange("g (q r) c -> r q g c", r=4)
    for r in range(4):
        nc.sync.dma_start(out=planes[r:P:32, :, :].bitcast(I32), in_=rows[r].bitcast(I32))


def tile_picked_ypagetb_max_po_kernel(
    tc, x_words, x_scales, w1_words, w1_scales, w2_words, w2_scales, unit, w3_words, w3_scales,
    offs, blk, tok, req, out_0, out_1, out_2,
):
    nc = tc.nc
    with ExitStack() as ctx:
        keep = ctx.enter_context(tc.tile_pool(name="keep", bufs=1))
        psum = ctx.enter_context(tc.psum_pool(name="psum", bufs=1))

        def sb(name, shape, dtype):
            return keep.tile(shape, dtype, name=name, align_bytes=64)

        offs_sb = sb("offs_sb", [P, S // 16], U16)
        blk_sb = sb("blk_sb", [P, V // 16], U16)
        tok_sb = sb("tok_sb", [P, U // 16], U16)
        req_sb = sb("req_sb", [P, U // 16], U16)
        unit_sb = sb("unit_sb", [P, PACK], F32)
        xw = [sb("xw%d" % g, [P, T], I32) for g in range(PASSES)]
        xs = sb("xs", [P, PASSES, T], U8)
        passes_of = {"w1": PASSES, "w2": PASSES, "w3": 1}
        ww_raw = {n: sb(n + "w_raw", [P, g, 2 * H], U8) for n, g in passes_of.items()}
        ww = {
            "w1": sb("w1w", [P, PACK, PASSES, 2 * P], U8)[:],
            "w2": sb("w2w", [P, PASSES, PACK, 2 * P], U8)[:].rearrange("p g t m -> p t g m"),
            "w3": sb("w3w", [P, PACK, 1, 2 * P], U8)[:],
        }
        s21_raw = sb("s21_raw", [P, 2 * PASSES, H], U8)
        s3_raw = sb("s3_raw", [P, 1, H], U8)
        s_first = sb("s_first", [P, PACK, P], U8)
        s_rest = sb("s_rest", [P, PACK, 2 * PASSES - 1, P], U8)
        s3 = sb("s3", [P, PACK, P], U8)

        nc.gpsimd.memset(s21_raw[:, :PASSES, :].bitcast(I32), 0)
        nc.vector.memset(xs[:].bitcast(I32), 0)
        nc.vector.memset(s21_raw[:, PASSES:, :].bitcast(I32), 0)
        nc.vector.memset(s3_raw[:].bitcast(I32), 0)

        def load_words(n, w):
            nc.sync.dma_start(out=ww_raw[n][:].bitcast(I32), in_=w.rearrange("g p c -> p g c").bitcast(I32))

        def load_x(g):
            nc.sync.dma_start(out=xw[g][:], in_=x_words[g].rearrange("p c r -> p (c r)").bitcast(I32))

        nc.sync.dma_start(offs_sb[:], offs)
        nc.scalar.dma_start(out=unit_sb[:], in_=unit.rearrange("(p t) o -> p (t o)", t=PACK))
        load_scale_rows(nc, s21_raw[:, :PASSES, :], w2_scales)
        load_x(0)
        load_words("w2", w2_words)
        load_scale_rows(nc, xs, x_scales)
        load_x(1)
        load_words("w1", w1_words)
        load_scale_rows(nc, s21_raw[:, PASSES:, :], w1_scales)
        nc.sync.dma_start(blk_sb[:], blk)
        nc.sync.dma_start(tok_sb[:], tok)
        load_words("w3", w3_words)
        nc.sync.dma_start(req_sb[:], req)
        load_scale_rows(nc, s3_raw, w3_scales)

        sign = sb("sign", [P, 2, 2], BF16)
        size = sb("size", [P, PACK], F32)
        nc.scalar.activation(size[:], unit_sb[:], ACT.Abs)
        nc.scalar.activation(sign[:].rearrange("p u e -> p (u e)"), unit_sb[:], ACT.Sign)

        def deal_words(n, ts, passes=slice(0, PASSES)):
            nc.scalar.copy(
                out=ww[n][:, ts, passes, :].bitcast(U16),
                in_=ww_raw[n][:].bitcast(U16).rearrange("p g (m t) -> p t g m", t=PACK)[:, ts, passes, :],
            )

        s21_dealt = s21_raw[:].rearrange("p g (m t) -> p t g m", t=PACK)

        def deal_rest(ts, first_plane, last_plane):
            nc.vector.tensor_copy(
                out=s_rest[:, ts, first_plane - 1 : last_plane, :], in_=s21_dealt[:, ts, first_plane : last_plane + 1, :]
            )

        gw = [sb("gw%d" % g, [P, S], U32) for g in range(PASSES)]
        gs = [sb("gs%d" % g, [P, S], U8) for g in range(PASSES)]

        def gather_words(g):
            nc.vector.tensor_copy(gw[g][:], xw[g][:].bitcast(U32).indirect(offs_sb[:]))

        def gather_scales(g):
            nc.vector.tensor_copy(gs[g][:], xs[:, g, :].indirect(offs_sb[:]))

        nc.vector.tensor_copy(out=s_first[:], in_=s21_dealt[:, :, 0, :])
        deal_rest(slice(0, 1), 1, 1)
        deal_words("w2", slice(0, PACK), slice(0, 1))
        deal_words("w2", slice(0, PACK), slice(1, 2))
        gather_words(0)
        gather_scales(0)
        gather_scales(1)
        gather_words(1)
        deal_rest(slice(0, 1), 2, 3)
        deal_words("w1", slice(0, 1))
        for ts in (slice(1, 2), slice(2, PACK)):
            deal_rest(ts, 1, 3)
            deal_words("w1", ts)

        acc = {}
        for t in range(PACK):
            for n in ("w2", "w1"):
                acc[n, t] = psum.tile([P, S], F32, name="acc_%s_%d" % (n, t), tag="bank_%s_%d" % (n, t))

        def product_pass(n, t, g):
            plane = g if n == "w2" else PASSES + g
            nc.tensor.matmul_mx(
                out=acc[n, t][:],
                lhsT=ww[n][:, t, g, :].bitcast(FP4X4),
                lhsT_scale=s_first[:, t, :] if plane == 0 else s_rest[:, t, plane - 1, :],
                rhs=gw[g][:].bitcast(FP8X4),
                rhs_scale=gs[g][:],
                start=(g == 0),
                stop=(g == PASSES - 1),
            )

        for t in range(PACK):
            product_pass("w2", t, 0)
        for t in range(PACK):
            product_pass("w2", t, 1)
            product_pass("w1", t, 0)
            product_pass("w1", t, 1)

        bounded = [sb("bounded%d" % t, [P, S], F32) for t in range(PACK)]
        pages = [sb("pages%d" % t, [P, V + S], F32) for t in range(PACK)]
        tk = [sb("tk%d" % u, [P, 2, U], F32) for u in range(2)]
        copy_on = {"V": nc.vector.tensor_copy, "S": lambda o, i: nc.scalar.activation(o, i, ACT.Copy)}

        for t in range(PACK):
            nc.scalar.activation(bounded[t][:], acc["w2", t][:], ACT.Tanh)
        for t in range(PACK):
            nc.vector.scalar_tensor_tensor(
                pages[t][:, V:], acc["w1", t][:], size[:, t : t + 1], bounded[t][:], ALU.mult, ALU.mult
            )
            copy_on[BLK_ON[t]](pages[t][:, :V], pages[t][:, V:].indirect(blk_sb[:]))
        for t in range(PACK):
            copy_on[TOK_ON[t]](tk[t // 2][:, t % 2, :], pages[t][:].indirect(tok_sb[:]))

        deal_words("w3", slice(0, PACK), slice(0, 1))
        nc.vector.tensor_copy(out=s3[:], in_=s3_raw[:, 0, :].rearrange("p (m t) -> p t m", t=PACK))

        out_words = sb("out_words", [P, U], U32)
        out_scales = sb("out_scales", [P, U], U8)
        out_rows = out_0.rearrange("(p t) j -> p t j", t=PACK)
        words_dram = out_1[0].rearrange("p c r -> p (c r)").bitcast(I32)
        free_banks = ["bank_%s_%d" % (n, t) for t in range(PACK) for n in ("w2", "w1")]
        starts = [sum(WIDTHS[:q]) for q in range(len(WIDTHS))]
        results = {}
        others = {}

        def front(q):
            width = WIDTHS[q]
            cols = slice(starts[q], starts[q] + width)
            if q % 2 == 0:
                picks = req_sb[:, cols.start // 16 : (cols.start + 2 * width) // 16]
                others[q // 2] = sb("other%d" % q, [P, PACK, 2 * width], F32)
                for t in range(PACK):
                    nc.scalar.activation(
                        others[q // 2][:, t, :], tk[t // 2][:, t % 2, :].indirect(picks), ACT.Copy, scale=-0.8
                    )
            other = others[q // 2][:, :, q % 2 * width : (q % 2 + 1) * width]
            pairs = sb("pairs%d" % q, [P, 2, width, 2], BF16)
            for u in range(2):
                nc.vector.tensor_tensor(
                    pairs[:, u, :, :].rearrange("p (c i) e -> p c e i", i=4),
                    other[:, 2 * u : 2 * u + 2, :].rearrange("p e (c i) -> p c e i", i=4),
                    tk[u][:, :, cols].rearrange("p e (c i) -> p c e i", i=4),
                    ALU.max,
                )
            hid = sb("hid%d" % q, [P, width, 2, 2], BF16)
            nc.vector.tensor_tensor(
                hid[:],
                pairs[:].rearrange("p u c e -> p c u e"),
                sign[:].unsqueeze(1).to_broadcast([P, width, 2, 2]),
                ALU.mult,
            )
            hid_words = sb("hid_words%d" % q, [P, width], U32)
            hid_scales = sb("hid_scales%d" % q, [P, width], U8)
            nc.vector.quantize_mx(
                out=hid_words[:].bitcast(FP8X4), scales=hid_scales[:], in_=hid[:].rearrange("p c u e -> p (c u e)")
            )
            per_bank = BANK // width
            results[q] = []
            for t0 in range(0, PACK, per_bank):
                res = psum.tile([P, per_bank, width], F32, name="res%d_%d" % (q, t0), tag=free_banks.pop(0))
                results[q].append(res)
                for t in range(t0, t0 + per_bank):
                    nc.tensor.matmul_mx(
                        out=res[:, t - t0, :],
                        lhsT=ww["w3"][:, t, 0, :].bitcast(FP4X4),
                        lhsT_scale=s3[:, t, :],
                        rhs=hid_words[:].bitcast(FP8X4),
                        rhs_scale=hid_scales[:],
                        start=True,
                        stop=True,
                    )

        def back(q):
            width = WIDTHS[q]
            cols = slice(starts[q], starts[q] + width)
            per_bank = BANK // width
            res32 = sb("res32_%d" % q, [P, PACK, width], F32)
            res16 = sb("res16_%d" % q, [P, width, PACK], BF16)
            for i, res in enumerate(results[q]):
                if ROUND_ON[q] == "S":
                    nc.scalar.copy(res16[:], res[:].rearrange("p t c -> p c t"))
                nc.scalar.copy(res32[:, i * per_bank : (i + 1) * per_bank, :], res[:])
            nc.sync.dma_start(out=out_rows[:, :, cols], in_=res32[:])
            if ROUND_ON[q] == "V":
                nc.vector.tensor_copy(
                    res16[:].rearrange("p (c i) t -> p c t i", i=4), res32[:].rearrange("p t (c i) -> p c t i", i=4)
                )
            nc.vector.quantize_mx(
                out=out_words[:, cols].bitcast(FP8X4), scales=out_scales[:, cols], in_=res16[:].rearrange("p c t -> p (c t)")
            )
            nc.sync.dma_start(out=words_dram[:, cols], in_=out_words[:, cols].bitcast(I32))

        for q in range(len(WIDTHS)):
            front(q)
        for q in range(len(WIDTHS)):
            back(q)
        scale_rows = out_2[0].rearrange("(q r) c -> r q c", r=4)
        for r in range(4):
            (nc.sync if r % 2 else nc.scalar).dma_start(
                out=scale_rows[r].bitcast(I32), in_=out_scales[r:P:32, :].bitcast(I32)
            )
